import numpy as np
import ml_dtypes


def mxq(x, axis, fmt="e4m3"):
    dtype, down = {"e4m3": (ml_dtypes.float8_e4m3fn, 7), "e5m2": (ml_dtypes.float8_e5m2, 14)}[fmt]
    v = np.moveaxis(np.asarray(x, np.float32).astype(ml_dtypes.bfloat16).astype(np.float64), axis, -1)
    blocks = v.reshape(v.shape[:-1] + (-1, 32))
    amax = np.abs(blocks).max(-1, keepdims=True)
    byte = np.maximum(np.where(amax > 0, np.frexp(amax)[1] - 1 + 127, 0) - down, 1)
    scale = np.exp2(byte - 127.0)
    codes = (blocks / scale).astype(np.float32).astype(dtype).astype(np.float64)
    return np.moveaxis((codes * scale).reshape(v.shape), -1, axis)


WIDE = False


def mx_kscale(k):
    if not WIDE:
        return np.ones(k)
    levels = np.array([10, -10, 5, -5, 0])
    if k % 512:
        return np.exp2(np.random.permutation(np.resize(levels, k // 32))).repeat(32)
    a = np.empty((k // 512, 16))
    for p in range(k // 512):
        a[p, :8] = np.random.permutation(np.resize(levels, 8))
        for g in range(8):
            far = levels[np.abs(levels - a[p, g]) >= 10]
            a[p, g + 8] = far[np.random.randint(len(far))]
    return np.exp2(a.ravel()).repeat(32)


def f64(x):
    return np.asarray(x).astype(np.float64)


def striped(idx):
    return np.tile(idx.reshape(-1, 16).T, (8, 1)).astype(np.uint16)


def unstriped(offs):
    return offs[:16].T.reshape(-1).astype(np.int64)


def striped8(idx):
    return np.concatenate([x.reshape(-1, 16).T for x in idx]).astype(np.uint16)


def runs(offs, k):
    lists = np.stack([offs[16 * r : 16 * r + 16].T.reshape(-1) for r in range(8)]).astype(np.int64)
    return lists[np.arange(k) % 512 // 64]


def pack_weight(w):
    k, n = w.shape
    w = f64(np.asarray(w, np.float32).astype(ml_dtypes.bfloat16)).reshape(k // 32, 32, n)
    amax = np.abs(w).max(1)
    byte = np.clip(np.where(amax > 0, np.frexp(amax)[1] - 1 + 127 - 7, 1), 1, 254)
    scaled = (w * np.exp2(127.0 - byte)[:, None, :]).reshape(k, n).astype(np.float32)
    words = np.ascontiguousarray(scaled.reshape(k // 512, 128, 4, n).transpose(0, 1, 3, 2)).astype(ml_dtypes.float8_e4m3fn).view(np.uint8)
    return words, np.ascontiguousarray(byte.astype(np.uint8).reshape(k // 512, 16, n))


def unpack_weight(words, scales):
    g, p, n, _ = words.shape
    vals = np.ascontiguousarray(words).view(ml_dtypes.float8_e4m3fn).astype(np.float64) * np.repeat(np.exp2(scales.astype(np.float64) - 127.0), 8, axis=1)[..., None]
    return vals.transpose(0, 1, 3, 2).reshape(g * 512, n)


def sigmoid(v):
    return 1.0 / (1.0 + np.exp(-np.maximum(v, -700.0)))


K, T, S, N, G, H = 512, 1024, 256, 512, 2048, 512


def setup_inputs():
    n = np.random.standard_normal
    s = mx_kscale(K)[:, None]
    u = mx_kscale(K)
    packed_xT = pack_weight(n((K, T)) * s)
    packed_dT = pack_weight(n((K, G)) / s)
    return {
        "x_words": packed_xT[0],
        "x_scales": packed_xT[1],
        "d_words": packed_dT[0],
        "d_scales": packed_dT[1],
        "tau": np.random.uniform(0.3, 0.9, (H, 1)).astype(np.float32),
        "gn": (np.random.uniform(0.5, 1.5, (H, 1)) * u[:, None]).astype(np.float32),
        "w1": (n((H, N)) / np.sqrt(H) / u[:, None]).astype(np.float32),
        "sl": np.random.uniform(1.5, 2.5, (N, 1)).astype(np.float32),
        "lo": np.random.uniform(-1.2, -0.4, (N, 1)).astype(np.float32),
        "hi": np.random.uniform(0.4, 1.2, (N, 1)).astype(np.float32),
        "offs": striped(np.random.permutation(T)[:S]),
        "k1": striped8(np.random.randint(0, G, (8, H))),
        "two": striped(np.random.permutation(T)[:S]),
        "k2": striped8(np.random.randint(0, G, (8, H))),
        "n1": striped(np.random.permutation(S)),
        "n2": striped(np.random.permutation(S)),
        "n3": striped8(np.stack([np.random.permutation(S) for _ in range(8)])),
    }


def reference(x_words, x_scales, d_words, d_scales, tau, gn, w1, sl, lo, hi, offs, k1, two, k2, n1, n2, n3):
    d_k1 = unpack_weight(d_words, d_scales)[np.arange(K)[:, None], runs(k1, K)]
    xq = unpack_weight(x_words, x_scales)[:, unstriped(offs)]
    a = 0.0625 * (d_k1.T @ xq)
    d_k2 = unpack_weight(d_words, d_scales)[np.arange(K)[:, None], runs(k2, K)]
    x_two = unpack_weight(x_words, x_scales)[:, unstriped(two)]
    b = 0.0625 * (d_k2.T @ x_two)
    top = b.max(axis=1, keepdims=True)
    ea = np.exp(f64(tau) * (b[:, unstriped(n1)] - top))
    z = f64(gn) * ((0.5 * (a - a[:, unstriped(n2)])) / (ea + 0.25))
    h = mxq(f64(w1), 0, "e4m3").T @ mxq(z, 0, "e4m3")
    sg = sigmoid(f64(sl) * (h[np.arange(N)[:, None], runs(n3, N)] - f64(lo)))
    sg2 = sigmoid(f64(sl) * (h[np.arange(N)[:, None], runs(n3, N)] - f64(hi)))
    return h * (sg - sg2)

@@ -1,0 +1,210 @@
+from contextlib import ExitStack
+
+import concourse.mybir as mybir
+
+K, T, S, N, G, H = 512, 1024, 256, 512, 2048, 512
+FLOPS = 2 * K * H * S * 2 + 2 * H * N * S
+
+F32 = mybir.dt.float32
+BF16 = mybir.dt.bfloat16
+I32 = mybir.dt.int32
+U32 = mybir.dt.uint32
+U16 = mybir.dt.uint16
+U8 = mybir.dt.uint8
+FP8X4 = mybir.dt.float8_e4m3fn_x4
+ALU = mybir.AluOpType
+ACT = mybir.ActivationFunctionType
+
+P = 128
+PACK = 4
+
+
+def tile_picked_twpqqxbebd_none_p_kernel(
+    tc, x_words, x_scales, d_words, d_scales, tau, gn, w1, sl, lo, hi, offs, k1, two, k2, n1, n2, n3, out
+):
+    nc = tc.nc
+    with ExitStack() as ctx:
+        lists = ctx.enter_context(tc.tile_pool(name="lists", bufs=1))
+        sb = ctx.enter_context(tc.tile_pool(name="sb", bufs=1))
+        ps = ctx.enter_context(tc.psum_pool(name="ps", bufs=1))
+
+        def load_list(name, src):
+            tile = lists.tile(list(src.shape), U16, name=name)
+            nc.sync.dma_start(tile[:], src)
+            return tile
+
+        def load_rows(name, src):
+            tile = sb.tile([P, PACK], F32, name=name)
+            nc.gpsimd.dma_start(tile[:], src.rearrange("(p t) o -> p (t o)", t=PACK))
+            return tile
+
+        def load_scales(name, src, width):
+            tile = sb.tile([P, width], U8, name=name, align_bytes=64)
+            nc.scalar.dma_start(tile[:].bitcast(I32), src[0].bitcast(I32).unsqueeze(1).broadcast_to([16, 8, width // 4]))
+            return tile
+
+        def load_words(name, src, width):
+            tile = sb.tile([P, width], U32, name=name, align_bytes=64)
+            nc.scalar.dma_start(tile[:].bitcast(I32), src[0].rearrange("p n r -> p (n r)").bitcast(I32))
+            return tile
+
+        d_sc = load_scales("d_sc", d_scales, G)
+        k2_l = load_list("k2_l", k2)
+        x_sc = load_scales("x_sc", x_scales, T)
+        two_l = load_list("two_l", two)
+        d_wd = load_words("d_wd", d_words, G)
+        k1_l = load_list("k1_l", k1)
+        offs_l = load_list("offs_l", offs)
+        x_wd = load_words("x_wd", x_words, T)
+        n1_l = load_list("n1_l", n1)
+        n2_l = load_list("n2_l", n2)
+        n3_l = load_list("n3_l", n3)
+        tau_t = load_rows("tau_t", tau)
+        gn_t = load_rows("gn_t", gn)
+        sl_t = load_rows("sl_t", sl)
+        lo_t = load_rows("lo_t", lo)
+        hi_t = load_rows("hi_t", hi)
+
+        row_win = [sb.tile([P, 2 * S], F32, name="row_win%d" % t) for t in range(PACK)]
+        for t in range(PACK):
+            nc.vector.memset(row_win[t][:, S:], 0.0)
+        a_win = sb.tile([P, (PACK + 1) * S], F32, name="a_win")
+        nc.vector.memset(a_win[:, PACK * S :], 0.0)
+
+        def pick_scales(name, d_list, x_list, got_tag):
+            got = sb.tile([P, H + S], U8, name=name + "_got", tag=got_tag, align_bytes=64)
+            plane = sb.tile([P, H + S], U8, name=name + "_plane", align_bytes=64)
+            nc.vector.tensor_copy(got[:, :H], d_sc[:].indirect(d_list[:]))
+            nc.vector.tensor_copy(got[:, H:], x_sc[:].indirect(x_list[:]))
+            nc.vector.tensor_copy(
+                plane[:, :H].rearrange("p (t c i) -> p c t i", t=PACK, i=16),
+                got[:, :H].rearrange("p (c i t) -> p c t i", t=PACK, i=16),
+            )
+            nc.vector.tensor_copy(plane[:, H:].bitcast(I32), got[:, H:].bitcast(I32))
+            for c in range(1, 4):
+                nc.sync.dma_start(plane[c:P:32, :].bitcast(I32), plane[8 * c : P : 32, :].bitcast(I32))
+            return plane
+
+        def pick_words(name, d_list, x_list, d_tag, dealt_tag):
+            d_got = sb.tile([P, H], U32, name=name + "_dwords", tag=d_tag, align_bytes=64)
+            dealt = sb.tile([P, H], U32, name=name + "_dealt", tag=dealt_tag, align_bytes=64)
+            x_got = sb.tile([P, S], U32, name=name + "_xwords", tag="xwords", align_bytes=64)
+            nc.vector.tensor_copy(d_got[:], d_wd[:].indirect(d_list[:]))
+            nc.vector.tensor_copy(x_got[:], x_wd[:].indirect(x_list[:]))
+            nc.vector.tensor_copy(
+                dealt[:].rearrange("p (t c i) -> p c t i", t=PACK, i=4),
+                d_got[:].rearrange("p (c i t) -> p c t i", t=PACK, i=4),
+            )
+            return dealt, x_got
+
+        def product(name, dealt, x_got, plane):
+            banks = [ps.tile([P, 2 * S], F32, name="%s_bank%d" % (name, u)) for u in range(2)]
+            sums = [banks[t // 2][:, (t % 2) * S : (t % 2 + 1) * S] for t in range(PACK)]
+            for t in range(PACK):
+                cols = slice(t * P, (t + 1) * P)
+                nc.tensor.matmul_mx(
+                    out=sums[t], lhsT=dealt[:, cols].bitcast(FP8X4), lhsT_scale=plane[:, cols],
+                    rhs=x_got[:].bitcast(FP8X4), rhs_scale=plane[:, H:], start=True, stop=True,
+                )
+            return sums
+
+        b_plane = pick_scales("b", k2_l, two_l, "first")
+        w_raw = sb.tile([P, PACK, N], F32, name="w_raw", tag="first", align_bytes=64)
+        nc.scalar.dma_start(w_raw[:], w1.rearrange("(p j) m -> p j m", j=PACK))
+        b_dealt, b_x = pick_words("b", k2_l, two_l, "second", "third")
+        b_sums = product("b", b_dealt, b_x, b_plane)
+        a_plane = pick_scales("a", k1_l, offs_l, "second")
+
+        top = sb.tile([P, PACK], F32, name="top")
+        exp_bias = sb.tile([P, PACK], F32, name="exp_bias")
+        ea = sb.tile([P, PACK, S], F32, name="ea")
+        for t in range(PACK):
+            nc.vector.tensor_scalar(
+                row_win[t][:, :S], b_sums[t], 0.0625, None, ALU.mult, ALU.max, accum_out=top[:, t : t + 1]
+            )
+        for t in range(PACK):
+            nc.vector.tensor_scalar(
+                exp_bias[:, t : t + 1], top[:, t : t + 1], tau_t[:, t : t + 1], -1.0, ALU.mult, ALU.mult
+            )
+            nc.scalar.activation(
+                ea[:, t, :], row_win[t][:].indirect(n1_l[:]), ACT.Exp,
+                bias=exp_bias[:, t : t + 1], scale=tau_t[:, t : t + 1],
+            )
+
+        a_dealt, a_x = pick_words("a", k1_l, offs_l, "third", "a_dealt")
+        a_sums = product("a", a_dealt, a_x, a_plane)
+
+        w_bf = sb.tile([P, PACK * N], BF16, name="w_bf", align_bytes=64)
+        for t in range(PACK):
+            nc.gpsimd.tensor_copy(
+                w_bf[:].rearrange("p (t m j) -> p t m j", t=PACK, j=PACK)[:, t],
+                w_raw[:].rearrange("p j (m t) -> p t m j", t=PACK)[:, t],
+            )
+        w_codes = sb.tile([P, N], U32, name="w_codes", tag="third", align_bytes=64)
+        w_plane = sb.tile([P, N], U8, name="w_plane", align_bytes=64)
+        nc.vector.quantize_mx(out=w_codes[:].bitcast(FP8X4), scales=w_plane[:], in_=w_bf[:])
+
+        gain = sb.tile([P, PACK], F32, name="gain")
+        nc.gpsimd.tensor_scalar(gain[:], gn_t[:], 0.5 * 0.0625, 0.0, ALU.mult, ALU.add)
+        neg_sl = sb.tile([P, PACK], F32, name="neg_sl")
+        nc.gpsimd.tensor_scalar(neg_sl[:], sl_t[:], -1.0, 0.0, ALU.mult, ALU.add)
+        lo_bias = sb.tile([P, PACK], F32, name="lo_bias")
+        hi_bias = sb.tile([P, PACK], F32, name="hi_bias")
+        nc.gpsimd.tensor_tensor(lo_bias[:], neg_sl[:], lo_t[:], ALU.mult)
+        nc.gpsimd.tensor_tensor(hi_bias[:], neg_sl[:], hi_t[:], ALU.mult)
+
+        def a_at(t):
+            return (PACK - 1 - t) * S
+
+        root = sb.tile([P, PACK, S], F32, name="root")
+        recip = sb.tile([P, PACK, S], F32, name="recip")
+        nc.scalar.activation(root[:], ea[:], ACT.Abs_reciprocal_sqrt, bias=0.25)
+        for t in range(PACK):
+            nc.scalar.activation(a_win[:, a_at(t) : a_at(t) + S], a_sums[t], ACT.Copy, scale=gain[:, t : t + 1])
+        nc.scalar.activation(recip[:], root[:], ACT.Square)
+
+        a_got = sb.tile([P, PACK, S], F32, name="a_got")
+        diff = sb.tile([P, PACK, S], F32, name="diff")
+        for t in range(PACK):
+            nc.vector.tensor_copy(a_got[:, t, :], a_win[:, a_at(t) : a_at(t) + 2 * S].indirect(n2_l[:]))
+        for t in range(PACK):
+            nc.vector.scalar_tensor_tensor(
+                diff[:, t, :], a_sums[t], gain[:, t : t + 1], a_got[:, t, :], ALU.mult, ALU.subtract
+            )
+
+        z_bf = sb.tile([P, PACK * S], BF16, name="z_bf", align_bytes=64)
+        nc.vector.tensor_tensor(
+            z_bf[:].rearrange("p (c i t) -> p c t i", t=PACK, i=4),
+            diff[:].rearrange("p t (c i) -> p c t i", i=4),
+            recip[:].rearrange("p t (c i) -> p c t i", i=4),
+            ALU.mult,
+        )
+        z_codes = sb.tile([P, S], U32, name="z_codes", align_bytes=64)
+        z_plane = sb.tile([P, S], U8, name="z_plane", align_bytes=64)
+        nc.vector.quantize_mx(out=z_codes[:].bitcast(FP8X4), scales=z_plane[:], in_=z_bf[:])
+
+        out_rows = out.rearrange("(p t) j -> p t j", t=PACK)
+        h_sums = [ps.tile([P, S], F32, name="h_bank%d" % t) for t in range(PACK)]
+        for t in range(PACK):
+            cols = slice(t * P, (t + 1) * P)
+            nc.tensor.matmul_mx(
+                out=h_sums[t][:], lhsT=w_codes[:, cols].bitcast(FP8X4), lhsT_scale=w_plane[:, cols],
+                rhs=z_codes[:].bitcast(FP8X4), rhs_scale=z_plane[:], start=True, stop=True,
+            )
+        for t in range(PACK):
+            nc.vector.tensor_copy(row_win[t][:, :S], h_sums[t][:])
+        for t in range(PACK):
+            sg = sb.tile([P, S], F32, name="sg%d" % t)
+            sg2 = sb.tile([P, S], F32, name="sg2%d" % t)
+            band = sb.tile([P, S], F32, name="band%d" % t)
+            result = sb.tile([P, S], F32, name="result%d" % t)
+            slope = sl_t[:, t : t + 1]
+            nc.scalar.activation(
+                sg[:], row_win[t][:].indirect(n3_l[:]), ACT.Sigmoid, bias=lo_bias[:, t : t + 1], scale=slope
+            )
+            nc.scalar.activation(
+                sg2[:], row_win[t][:].indirect(n3_l[:]), ACT.Sigmoid, bias=hi_bias[:, t : t + 1], scale=slope
+            )
+            nc.vector.tensor_tensor(band[:], sg[:], sg2[:], ALU.subtract)
+            nc.vector.tensor_tensor(result[:], band[:], h_sums[t][:], ALU.mult)
+            nc.sync.dma_start(out_rows[:, t, :], result[:])

@@ -33,37 +33,32 @@ def tile_picked_twpqqxbebd_none_p_kernel(
             nc.sync.dma_start(tile[:], src)
             return tile
 
-        def load_rows(name, src):
-            tile = sb.tile([P, PACK], F32, name=name)
-            nc.gpsimd.dma_start(tile[:], src.rearrange("(p t) o -> p (t o)", t=PACK))
-            return tile
+        def load_rows(dst, src):
+            nc.sync.dma_start(dst, src.rearrange("(p t) o -> p (t o)", t=PACK))
+            return dst
 
         def load_scales(name, src, width):
             tile = sb.tile([P, width], U8, name=name, align_bytes=64)
-            nc.scalar.dma_start(tile[:].bitcast(I32), src[0].bitcast(I32).unsqueeze(1).broadcast_to([16, 8, width // 4]))
+            nc.sync.dma_start(tile[:].bitcast(I32), src[0].bitcast(I32).unsqueeze(1).broadcast_to([16, 8, width // 4]))
             return tile
 
         def load_words(name, src, width):
             tile = sb.tile([P, width], U32, name=name, align_bytes=64)
-            nc.scalar.dma_start(tile[:].bitcast(I32), src[0].rearrange("p n r -> p (n r)").bitcast(I32))
+            nc.sync.dma_start(tile[:].bitcast(I32), src[0].rearrange("p n r -> p (n r)").bitcast(I32))
             return tile
 
         d_sc = load_scales("d_sc", d_scales, G)
         k2_l = load_list("k2_l", k2)
         x_sc = load_scales("x_sc", x_scales, T)
         two_l = load_list("two_l", two)
-        d_wd = load_words("d_wd", d_words, G)
         k1_l = load_list("k1_l", k1)
         offs_l = load_list("offs_l", offs)
+        d_wd = load_words("d_wd", d_words, G)
         x_wd = load_words("x_wd", x_words, T)
+        tau_t = load_rows(sb.tile([P, PACK], F32, name="tau_t")[:], tau)
         n1_l = load_list("n1_l", n1)
         n2_l = load_list("n2_l", n2)
         n3_l = load_list("n3_l", n3)
-        tau_t = load_rows("tau_t", tau)
-        gn_t = load_rows("gn_t", gn)
-        sl_t = load_rows("sl_t", sl)
-        lo_t = load_rows("lo_t", lo)
-        hi_t = load_rows("hi_t", hi)
 
         row_win = [sb.tile([P, 2 * S], F32, name="row_win%d" % t) for t in range(PACK)]
         for t in range(PACK):
@@ -71,24 +66,25 @@ def tile_picked_twpqqxbebd_none_p_kernel(
         a_win = sb.tile([P, (PACK + 1) * S], F32, name="a_win")
         nc.vector.memset(a_win[:, PACK * S :], 0.0)
 
-        def pick_scales(name, d_list, x_list, got_tag):
-            got = sb.tile([P, H + S], U8, name=name + "_got", tag=got_tag, align_bytes=64)
+        def pick_scales(name, d_list, x_list, d_tag, x_tag, queue):
+            d_got = sb.tile([P, H], U8, name=name + "_dbytes", tag=d_tag, align_bytes=64)
+            x_got = sb.tile([P, S], U8, name=name + "_xbytes", tag=x_tag, align_bytes=64)
             plane = sb.tile([P, H + S], U8, name=name + "_plane", align_bytes=64)
-            nc.vector.tensor_copy(got[:, :H], d_sc[:].indirect(d_list[:]))
-            nc.vector.tensor_copy(got[:, H:], x_sc[:].indirect(x_list[:]))
+            nc.vector.tensor_copy(d_got[:], d_sc[:].indirect(d_list[:]))
+            nc.vector.tensor_copy(x_got[:], x_sc[:].indirect(x_list[:]))
             nc.vector.tensor_copy(
                 plane[:, :H].rearrange("p (t c i) -> p c t i", t=PACK, i=16),
-                got[:, :H].rearrange("p (c i t) -> p c t i", t=PACK, i=16),
+                d_got[:].rearrange("p (c i t) -> p c t i", t=PACK, i=16),
             )
-            nc.vector.tensor_copy(plane[:, H:].bitcast(I32), got[:, H:].bitcast(I32))
+            nc.vector.tensor_copy(plane[:, H:].bitcast(I32), x_got[:].bitcast(I32))
             for c in range(1, 4):
-                nc.sync.dma_start(plane[c:P:32, :].bitcast(I32), plane[8 * c : P : 32, :].bitcast(I32))
+                queue.dma_start(plane[c:P:32, :].bitcast(I32), plane[8 * c : P : 32, :].bitcast(I32))
             return plane
 
-        def pick_words(name, d_list, x_list, d_tag, dealt_tag):
+        def pick_words(name, d_list, x_list, d_tag, dealt_tag, x_tag):
             d_got = sb.tile([P, H], U32, name=name + "_dwords", tag=d_tag, align_bytes=64)
             dealt = sb.tile([P, H], U32, name=name + "_dealt", tag=dealt_tag, align_bytes=64)
-            x_got = sb.tile([P, S], U32, name=name + "_xwords", tag="xwords", align_bytes=64)
+            x_got = sb.tile([P, S], U32, name=name + "_xwords", tag=x_tag, align_bytes=64)
             nc.vector.tensor_copy(d_got[:], d_wd[:].indirect(d_list[:]))
             nc.vector.tensor_copy(x_got[:], x_wd[:].indirect(x_list[:]))
             nc.vector.tensor_copy(
@@ -98,8 +94,7 @@ def tile_picked_twpqqxbebd_none_p_kernel(
             return dealt, x_got
 
         def product(name, dealt, x_got, plane):
-            banks = [ps.tile([P, 2 * S], F32, name="%s_bank%d" % (name, u)) for u in range(2)]
-            sums = [banks[t // 2][:, (t % 2) * S : (t % 2 + 1) * S] for t in range(PACK)]
+            sums = [ps.tile([P, S], F32, name="%s_bank%d" % (name, t), tag="%s%d" % (name, t))[:] for t in range(PACK)]
             for t in range(PACK):
                 cols = slice(t * P, (t + 1) * P)
                 nc.tensor.matmul_mx(
@@ -108,12 +103,16 @@ def tile_picked_twpqqxbebd_none_p_kernel(
                 )
             return sums
 
-        b_plane = pick_scales("b", k2_l, two_l, "first")
-        w_raw = sb.tile([P, PACK, N], F32, name="w_raw", tag="first", align_bytes=64)
-        nc.scalar.dma_start(w_raw[:], w1.rearrange("(p j) m -> p j m", j=PACK))
-        b_dealt, b_x = pick_words("b", k2_l, two_l, "second", "third")
+        b_plane = pick_scales("b", k2_l, two_l, "b_dbytes", "first", nc.scalar)
+        late = sb.tile([P, PACK * N + 32], F32, name="late", tag="first", align_bytes=64)
+        w_raw = late[:, : PACK * N].rearrange("p (j m) -> p j m", j=PACK)
+        rows = late[:, PACK * N :].rearrange("p (u c) -> p u c", c=8)
+        gn_t, sl_t, lo_t, hi_t = [
+            load_rows(rows[:, u, :PACK], src) for u, src in enumerate((gn, sl, lo, hi))
+        ]
+        nc.sync.dma_start(w_raw, w1.rearrange("(p j) m -> p j m", j=PACK))
+        b_dealt, b_x = pick_words("b", k2_l, two_l, "second", "third", "fourth")
         b_sums = product("b", b_dealt, b_x, b_plane)
-        a_plane = pick_scales("a", k1_l, offs_l, "second")
 
         top = sb.tile([P, PACK], F32, name="top")
         exp_bias = sb.tile([P, PACK], F32, name="exp_bias")
@@ -131,37 +130,35 @@ def tile_picked_twpqqxbebd_none_p_kernel(
                 bias=exp_bias[:, t : t + 1], scale=tau_t[:, t : t + 1],
             )
 
-        a_dealt, a_x = pick_words("a", k1_l, offs_l, "third", "a_dealt")
+        a_plane = pick_scales("a", k1_l, offs_l, "fourth", "second", nc.sync)
+        a_dealt, a_x = pick_words("a", k1_l, offs_l, "third", "a_dealt", "fourth")
         a_sums = product("a", a_dealt, a_x, a_plane)
 
-        w_bf = sb.tile([P, PACK * N], BF16, name="w_bf", align_bytes=64)
-        for t in range(PACK):
-            nc.gpsimd.tensor_copy(
-                w_bf[:].rearrange("p (t m j) -> p t m j", t=PACK, j=PACK)[:, t],
-                w_raw[:].rearrange("p j (m t) -> p t m j", t=PACK)[:, t],
-            )
-        w_codes = sb.tile([P, N], U32, name="w_codes", tag="third", align_bytes=64)
-        w_plane = sb.tile([P, N], U8, name="w_plane", align_bytes=64)
-        nc.vector.quantize_mx(out=w_codes[:].bitcast(FP8X4), scales=w_plane[:], in_=w_bf[:])
-
         gain = sb.tile([P, PACK], F32, name="gain")
-        nc.gpsimd.tensor_scalar(gain[:], gn_t[:], 0.5 * 0.0625, 0.0, ALU.mult, ALU.add)
+        nc.gpsimd.tensor_scalar(gain[:], gn_t, 8.0 * 0.5 * 0.0625, 0.0, ALU.mult, ALU.add)
         neg_sl = sb.tile([P, PACK], F32, name="neg_sl")
-        nc.gpsimd.tensor_scalar(neg_sl[:], sl_t[:], -1.0, 0.0, ALU.mult, ALU.add)
+        nc.gpsimd.tensor_scalar(neg_sl[:], sl_t, -1.0, 0.0, ALU.mult, ALU.add)
         lo_bias = sb.tile([P, PACK], F32, name="lo_bias")
         hi_bias = sb.tile([P, PACK], F32, name="hi_bias")
-        nc.gpsimd.tensor_tensor(lo_bias[:], neg_sl[:], lo_t[:], ALU.mult)
-        nc.gpsimd.tensor_tensor(hi_bias[:], neg_sl[:], hi_t[:], ALU.mult)
+        nc.gpsimd.tensor_tensor(lo_bias[:], neg_sl[:], lo_t, ALU.mult)
+        nc.gpsimd.tensor_tensor(hi_bias[:], neg_sl[:], hi_t, ALU.mult)
 
         def a_at(t):
             return (PACK - 1 - t) * S
 
         root = sb.tile([P, PACK, S], F32, name="root")
-        recip = sb.tile([P, PACK, S], F32, name="recip")
-        nc.scalar.activation(root[:], ea[:], ACT.Abs_reciprocal_sqrt, bias=0.25)
+        recip = sb.tile([P, PACK, S], F32, name="recip", tag="a_dealt", align_bytes=64)
+        nc.scalar.activation(root[:], ea[:], ACT.Ln, scale=8.0, bias=1.0)
         for t in range(PACK):
             nc.scalar.activation(a_win[:, a_at(t) : a_at(t) + S], a_sums[t], ACT.Copy, scale=gain[:, t : t + 1])
-        nc.scalar.activation(recip[:], root[:], ACT.Square)
+        nc.scalar.activation(recip[:], root[:], ACT.Sigmoid, scale=-1.0)
+
+        w_bf = sb.tile([P, PACK * N], BF16, name="w_bf", tag="third", align_bytes=64)
+        for t in range(PACK):
+            nc.gpsimd.tensor_copy(
+                w_bf[:].rearrange("p (t m j) -> p t m j", t=PACK, j=PACK)[:, t],
+                w_raw.rearrange("p j (m t) -> p t m j", t=PACK)[:, t],
+            )
 
         a_got = sb.tile([P, PACK, S], F32, name="a_got")
         diff = sb.tile([P, PACK, S], F32, name="diff")
@@ -172,6 +169,8 @@ def tile_picked_twpqqxbebd_none_p_kernel(
                 diff[:, t, :], a_sums[t], gain[:, t : t + 1], a_got[:, t, :], ALU.mult, ALU.subtract
             )
 
+        w_codes = sb.tile([P, N], U32, name="w_codes", align_bytes=64)
+        w_plane = sb.tile([P, N], U8, name="w_plane", align_bytes=64)
         z_bf = sb.tile([P, PACK * S], BF16, name="z_bf", align_bytes=64)
         nc.vector.tensor_tensor(
             z_bf[:].rearrange("p (c i t) -> p c t i", t=PACK, i=4),
@@ -183,8 +182,10 @@ def tile_picked_twpqqxbebd_none_p_kernel(
         z_plane = sb.tile([P, S], U8, name="z_plane", align_bytes=64)
         nc.vector.quantize_mx(out=z_codes[:].bitcast(FP8X4), scales=z_plane[:], in_=z_bf[:])
 
+        nc.vector.quantize_mx(out=w_codes[:].bitcast(FP8X4), scales=w_plane[:], in_=w_bf[:])
+
         out_rows = out.rearrange("(p t) j -> p t j", t=PACK)
-        h_sums = [ps.tile([P, S], F32, name="h_bank%d" % t) for t in range(PACK)]
+        h_sums = [ps.tile([P, S], F32, name="h_bank%d" % t, tag="b%d" % t) for t in range(PACK)]
         for t in range(PACK):
             cols = slice(t * P, (t + 1) * P)
             nc.tensor.matmul_mx(

@@ -49,11 +49,16 @@ def tile_picked_twpqqxbebd_none_p_kernel(
 
         d_sc = load_scales("d_sc", d_scales, G)
         k2_l = load_list("k2_l", k2)
-        x_sc = load_scales("x_sc", x_scales, T)
+        x_sc = sb.tile([P, T], U8, name="x_sc", align_bytes=64)
+        for q in range(4):
+            quad_rows = x_scales[0, 4 * q : 4 * q + 4, :].bitcast(I32)
+            nc.sync.dma_start(
+                x_sc[32 * q : 32 * (q + 1), :].bitcast(I32), quad_rows.unsqueeze(0).broadcast_to([8, 4, T // 4])
+            )
         two_l = load_list("two_l", two)
-        k1_l = load_list("k1_l", k1)
-        offs_l = load_list("offs_l", offs)
         d_wd = load_words("d_wd", d_words, G)
+        offs_l = load_list("offs_l", offs)
+        k1_l = load_list("k1_l", k1)
         x_wd = load_words("x_wd", x_words, T)
         tau_t = load_rows(sb.tile([P, PACK], F32, name="tau_t")[:], tau)
         n1_l = load_list("n1_l", n1)
@@ -66,62 +71,66 @@ def tile_picked_twpqqxbebd_none_p_kernel(
         a_win = sb.tile([P, (PACK + 1) * S], F32, name="a_win")
         nc.vector.memset(a_win[:, PACK * S :], 0.0)
 
-        def pick_scales(name, d_list, x_list, d_tag, x_tag, queue):
-            d_got = sb.tile([P, H], U8, name=name + "_dbytes", tag=d_tag, align_bytes=64)
-            x_got = sb.tile([P, S], U8, name=name + "_xbytes", tag=x_tag, align_bytes=64)
-            plane = sb.tile([P, H + S], U8, name=name + "_plane", align_bytes=64)
-            nc.vector.tensor_copy(d_got[:], d_sc[:].indirect(d_list[:]))
-            nc.vector.tensor_copy(x_got[:], x_sc[:].indirect(x_list[:]))
+        def deal_scales(name, d_list, tag, plane):
+            got = sb.tile([P, H], U8, name=name, tag=tag, align_bytes=64)
+            nc.vector.tensor_copy(got[:], d_sc[:].indirect(d_list[:]))
             nc.vector.tensor_copy(
                 plane[:, :H].rearrange("p (t c i) -> p c t i", t=PACK, i=16),
-                d_got[:].rearrange("p (c i t) -> p c t i", t=PACK, i=16),
+                got[:].rearrange("p (c i t) -> p c t i", t=PACK, i=16),
             )
-            nc.vector.tensor_copy(plane[:, H:].bitcast(I32), x_got[:].bitcast(I32))
+
+        def place_scale_rows(queue, plane):
             for c in range(1, 4):
                 queue.dma_start(plane[c:P:32, :].bitcast(I32), plane[8 * c : P : 32, :].bitcast(I32))
-            return plane
 
-        def pick_words(name, d_list, x_list, d_tag, dealt_tag, x_tag):
-            d_got = sb.tile([P, H], U32, name=name + "_dwords", tag=d_tag, align_bytes=64)
-            dealt = sb.tile([P, H], U32, name=name + "_dealt", tag=dealt_tag, align_bytes=64)
-            x_got = sb.tile([P, S], U32, name=name + "_xwords", tag=x_tag, align_bytes=64)
-            nc.vector.tensor_copy(d_got[:], d_wd[:].indirect(d_list[:]))
-            nc.vector.tensor_copy(x_got[:], x_wd[:].indirect(x_list[:]))
+        def deal_words(got, dealt):
             nc.vector.tensor_copy(
                 dealt[:].rearrange("p (t c i) -> p c t i", t=PACK, i=4),
-                d_got[:].rearrange("p (c i t) -> p c t i", t=PACK, i=4),
+                got.rearrange("p (c i t) -> p c t i", t=PACK, i=4),
             )
-            return dealt, x_got
 
-        def product(name, dealt, x_got, plane):
+        def product(name, dealt, d_plane, x_got, x_plane):
             sums = [ps.tile([P, S], F32, name="%s_bank%d" % (name, t), tag="%s%d" % (name, t))[:] for t in range(PACK)]
             for t in range(PACK):
                 cols = slice(t * P, (t + 1) * P)
                 nc.tensor.matmul_mx(
-                    out=sums[t], lhsT=dealt[:, cols].bitcast(FP8X4), lhsT_scale=plane[:, cols],
-                    rhs=x_got[:].bitcast(FP8X4), rhs_scale=plane[:, H:], start=True, stop=True,
+                    out=sums[t], lhsT=dealt[:, cols].bitcast(FP8X4), lhsT_scale=d_plane[:, cols],
+                    rhs=x_got.bitcast(FP8X4), rhs_scale=x_plane, start=True, stop=True,
                 )
             return sums
 
-        b_plane = pick_scales("b", k2_l, two_l, "b_dbytes", "first", nc.scalar)
-        late = sb.tile([P, PACK * N + 32], F32, name="late", tag="first", align_bytes=64)
-        w_raw = late[:, : PACK * N].rearrange("p (j m) -> p j m", j=PACK)
-        rows = late[:, PACK * N :].rearrange("p (u c) -> p u c", c=8)
+        b_plane = sb.tile([P, H], U8, name="b_plane", align_bytes=64)
+        deal_scales("b_dbytes", k2_l, "first", b_plane)
+        place_scale_rows(nc.scalar, b_plane)
+        x_bytes = sb.tile([P, 2 * S], U8, name="x_bytes", align_bytes=64)
+        nc.vector.tensor_copy(x_bytes[:, :S], x_sc[:].indirect(two_l[:]))
+        nc.vector.tensor_copy(x_bytes[:, S:], x_sc[:].indirect(offs_l[:]))
+
+        rows = sb.tile([P, 4, 8], F32, name="rows", tag="first", align_bytes=64)
         gn_t, sl_t, lo_t, hi_t = [
             load_rows(rows[:, u, :PACK], src) for u, src in enumerate((gn, sl, lo, hi))
         ]
-        nc.sync.dma_start(w_raw, w1.rearrange("(p j) m -> p j m", j=PACK))
-        b_dealt, b_x = pick_words("b", k2_l, two_l, "second", "third", "fourth")
-        b_sums = product("b", b_dealt, b_x, b_plane)
+
+        b_dwords = sb.tile([P, H], U32, name="b_dwords", tag="third", align_bytes=64)
+        b_xwords = sb.tile([P, S], U32, name="b_xwords", tag="second", align_bytes=64)
+        b_dealt = sb.tile([P, H], U32, name="b_dealt", tag="fourth", align_bytes=64)
+        nc.vector.tensor_copy(b_dwords[:], d_wd[:].indirect(k2_l[:]))
+        nc.vector.tensor_copy(b_xwords[:], x_wd[:].indirect(two_l[:]))
+        deal_words(b_dwords[:], b_dealt)
+        w_raw = sb.tile([P, PACK, N], F32, name="w_raw", tag="third", align_bytes=64)
+        nc.sync.dma_start(w_raw[:], w1.rearrange("(p j) m -> p j m", j=PACK))
+        b_sums = product("b", b_dealt, b_plane, b_xwords[:], x_bytes[:, :S])
 
         top = sb.tile([P, PACK], F32, name="top")
         exp_bias = sb.tile([P, PACK], F32, name="exp_bias")
         ea = sb.tile([P, PACK, S], F32, name="ea")
-        for t in range(PACK):
+
+        def empty_b(t):
             nc.vector.tensor_scalar(
                 row_win[t][:, :S], b_sums[t], 0.0625, None, ALU.mult, ALU.max, accum_out=top[:, t : t + 1]
             )
-        for t in range(PACK):
+
+        def fetch_exp(t):
             nc.vector.tensor_scalar(
                 exp_bias[:, t : t + 1], top[:, t : t + 1], tau_t[:, t : t + 1], -1.0, ALU.mult, ALU.mult
             )
@@ -130,9 +139,22 @@ def tile_picked_twpqqxbebd_none_p_kernel(
                 bias=exp_bias[:, t : t + 1], scale=tau_t[:, t : t + 1],
             )
 
-        a_plane = pick_scales("a", k1_l, offs_l, "fourth", "second", nc.sync)
-        a_dealt, a_x = pick_words("a", k1_l, offs_l, "third", "a_dealt", "fourth")
-        a_sums = product("a", a_dealt, a_x, a_plane)
+        empty_b(0)
+        for t in range(1, PACK):
+            empty_b(t)
+            fetch_exp(t - 1)
+        fetch_exp(PACK - 1)
+
+        a_plane = sb.tile([P, H], U8, name="a_plane", align_bytes=64)
+        deal_scales("a_dbytes", k1_l, "second", a_plane)
+        place_scale_rows(nc.sync, a_plane)
+        a_dwords = sb.tile([P, H], U32, name="a_dwords", tag="second", align_bytes=64)
+        a_xwords = sb.tile([P, S], U32, name="a_xwords", tag="fourth", align_bytes=64)
+        a_dealt = sb.tile([P, H], U32, name="a_dealt", tag="a_dealt", align_bytes=64)
+        nc.vector.tensor_copy(a_dwords[:], d_wd[:].indirect(k1_l[:]))
+        nc.vector.tensor_copy(a_xwords[:], x_wd[:].indirect(offs_l[:]))
+        deal_words(a_dwords[:], a_dealt)
+        a_sums = product("a", a_dealt, a_plane, a_xwords[:], x_bytes[:, S:])
 
         gain = sb.tile([P, PACK], F32, name="gain")
         nc.gpsimd.tensor_scalar(gain[:], gn_t, 8.0 * 0.5 * 0.0625, 0.0, ALU.mult, ALU.add)
@@ -143,22 +165,37 @@ def tile_picked_twpqqxbebd_none_p_kernel(
         nc.gpsimd.tensor_tensor(lo_bias[:], neg_sl[:], lo_t, ALU.mult)
         nc.gpsimd.tensor_tensor(hi_bias[:], neg_sl[:], hi_t, ALU.mult)
 
+        w_bf = {}
+
+        def round_weights(u, tag, copy):
+            w_bf[u] = sb.tile([P, 2 * N], BF16, name="w_bf%d" % u, tag=tag, align_bytes=64)
+            copy(
+                w_bf[u][:].rearrange("p (t m j) -> p m j t", t=2, j=PACK),
+                w_raw[:].rearrange("p j (m t) -> p m j t", t=PACK)[:, :, :, 2 * u : 2 * u + 2],
+            )
+
+        w_codes = sb.tile([P, N], U32, name="w_codes", align_bytes=64)
+        w_plane = sb.tile([P, N], U8, name="w_plane", align_bytes=64)
+
+        def quantize_weights(u):
+            cols = slice(2 * u * P, 2 * (u + 1) * P)
+            nc.vector.quantize_mx(out=w_codes[:, cols].bitcast(FP8X4), scales=w_plane[:, cols], in_=w_bf[u][:])
+
         def a_at(t):
             return (PACK - 1 - t) * S
 
-        root = sb.tile([P, PACK, S], F32, name="root")
+        root = sb.tile([P, PACK, S], F32, name="root", tag="root", align_bytes=64)
         recip = sb.tile([P, PACK, S], F32, name="recip", tag="a_dealt", align_bytes=64)
         nc.scalar.activation(root[:], ea[:], ACT.Ln, scale=8.0, bias=1.0)
+        round_weights(0, "second", nc.vector.tensor_copy)
+        quantize_weights(0)
         for t in range(PACK):
             nc.scalar.activation(a_win[:, a_at(t) : a_at(t) + S], a_sums[t], ACT.Copy, scale=gain[:, t : t + 1])
-        nc.scalar.activation(recip[:], root[:], ACT.Sigmoid, scale=-1.0)
+        halves = [slice(u * S // 2, (u + 1) * S // 2) for u in range(2)]
+        for cols in halves:
+            nc.scalar.activation(recip[:, :, cols], root[:, :, cols], ACT.Sigmoid, scale=-1.0)
 
-        w_bf = sb.tile([P, PACK * N], BF16, name="w_bf", tag="third", align_bytes=64)
-        for t in range(PACK):
-            nc.gpsimd.tensor_copy(
-                w_bf[:].rearrange("p (t m j) -> p t m j", t=PACK, j=PACK)[:, t],
-                w_raw.rearrange("p j (m t) -> p t m j", t=PACK)[:, t],
-            )
+        round_weights(1, "root", nc.scalar.copy)
 
         a_got = sb.tile([P, PACK, S], F32, name="a_got")
         diff = sb.tile([P, PACK, S], F32, name="diff")
@@ -169,20 +206,22 @@ def tile_picked_twpqqxbebd_none_p_kernel(
                 diff[:, t, :], a_sums[t], gain[:, t : t + 1], a_got[:, t, :], ALU.mult, ALU.subtract
             )
 
-        w_codes = sb.tile([P, N], U32, name="w_codes", align_bytes=64)
-        w_plane = sb.tile([P, N], U8, name="w_plane", align_bytes=64)
-        z_bf = sb.tile([P, PACK * S], BF16, name="z_bf", align_bytes=64)
-        nc.vector.tensor_tensor(
-            z_bf[:].rearrange("p (c i t) -> p c t i", t=PACK, i=4),
-            diff[:].rearrange("p t (c i) -> p c t i", i=4),
-            recip[:].rearrange("p t (c i) -> p c t i", i=4),
-            ALU.mult,
-        )
+        z_bf = sb.tile([P, S, PACK], BF16, name="z_bf", align_bytes=64)
         z_codes = sb.tile([P, S], U32, name="z_codes", align_bytes=64)
         z_plane = sb.tile([P, S], U8, name="z_plane", align_bytes=64)
-        nc.vector.quantize_mx(out=z_codes[:].bitcast(FP8X4), scales=z_plane[:], in_=z_bf[:])
-
-        nc.vector.quantize_mx(out=w_codes[:].bitcast(FP8X4), scales=w_plane[:], in_=w_bf[:])
+        for cols in halves:
+            nc.vector.tensor_tensor(
+                z_bf[:, cols, :].rearrange("p (c i) t -> p c t i", i=4),
+                diff[:, :, cols].rearrange("p t (c i) -> p c t i", i=4),
+                recip[:, :, cols].rearrange("p t (c i) -> p c t i", i=4),
+                ALU.mult,
+            )
+        for cols in halves:
+            nc.vector.quantize_mx(
+                out=z_codes[:, cols].bitcast(FP8X4), scales=z_plane[:, cols],
+                in_=z_bf[:, cols, :].rearrange("p j t -> p (j t)"),
+            )
+        quantize_weights(1)
 
         out_rows = out.rearrange("(p t) j -> p t j", t=PACK)
         h_sums = [ps.tile([P, S], F32, name="h_bank%d" % t, tag="b%d" % t) for t in range(PACK)]
@@ -203,9 +242,11 @@ def tile_picked_twpqqxbebd_none_p_kernel(
             nc.scalar.activation(
                 sg[:], row_win[t][:].indirect(n3_l[:]), ACT.Sigmoid, bias=lo_bias[:, t : t + 1], scale=slope
             )
-            nc.scalar.activation(
-                sg2[:], row_win[t][:].indirect(n3_l[:]), ACT.Sigmoid, bias=hi_bias[:, t : t + 1], scale=slope
-            )
-            nc.vector.tensor_tensor(band[:], sg[:], sg2[:], ALU.subtract)
-            nc.vector.tensor_tensor(result[:], band[:], h_sums[t][:], ALU.mult)
-            nc.sync.dma_start(out_rows[:, t, :], result[:])
+            for cols in halves if t == PACK - 1 else [slice(0, S)]:
+                places = n3_l[:, cols.start // 16 : cols.stop // 16]
+                nc.scalar.activation(
+                    sg2[:, cols], row_win[t][:].indirect(places), ACT.Sigmoid, bias=hi_bias[:, t : t + 1], scale=slope
+                )
+                nc.vector.tensor_tensor(band[:, cols], sg[:, cols], sg2[:, cols], ALU.subtract)
+                nc.vector.tensor_tensor(result[:, cols], band[:, cols], h_sums[t][:, cols], ALU.mult)
+                nc.sync.dma_start(out_rows[:, t, cols], result[:, cols])

from contextlib import ExitStack

import concourse.mybir as mybir

K, T, S, N, G, H = 512, 1024, 256, 512, 2048, 512
FLOPS = 2 * K * H * S * 2 + 2 * H * N * S

F32 = mybir.dt.float32
BF16 = mybir.dt.bfloat16
I32 = mybir.dt.int32
U32 = mybir.dt.uint32
U16 = mybir.dt.uint16
U8 = mybir.dt.uint8
FP8X4 = mybir.dt.float8_e4m3fn_x4
ALU = mybir.AluOpType
ACT = mybir.ActivationFunctionType

P = 128
PACK = 4


def tile_picked_twpqqxbebd_none_p_kernel(
    tc, x_words, x_scales, d_words, d_scales, tau, gn, w1, sl, lo, hi, offs, k1, two, k2, n1, n2, n3, out
):
    nc = tc.nc
    with ExitStack() as ctx:
        lists = ctx.enter_context(tc.tile_pool(name="lists", bufs=1))
        sb = ctx.enter_context(tc.tile_pool(name="sb", bufs=1))
        ps = ctx.enter_context(tc.psum_pool(name="ps", bufs=1))

        def load_list(name, src):
            tile = lists.tile(list(src.shape), U16, name=name)
            nc.sync.dma_start(tile[:], src)
            return tile

        def load_rows(dst, src):
            nc.sync.dma_start(dst, src.rearrange("(p t) o -> p (t o)", t=PACK))
            return dst

        def load_scales(name, src, width):
            tile = sb.tile([P, width], U8, name=name, align_bytes=64)
            nc.sync.dma_start(tile[:].bitcast(I32), src[0].bitcast(I32).unsqueeze(1).broadcast_to([16, 8, width // 4]))
            return tile

        def load_words(name, src, width):
            tile = sb.tile([P, width], U32, name=name, align_bytes=64)
            nc.sync.dma_start(tile[:].bitcast(I32), src[0].rearrange("p n r -> p (n r)").bitcast(I32))
            return tile

        d_sc = load_scales("d_sc", d_scales, G)
        k2_l = load_list("k2_l", k2)
        x_sc = sb.tile([P, T], U8, name="x_sc", align_bytes=64)
        for q in range(4):
            quad_rows = x_scales[0, 4 * q : 4 * q + 4, :].bitcast(I32)
            nc.sync.dma_start(
                x_sc[32 * q : 32 * (q + 1), :].bitcast(I32), quad_rows.unsqueeze(0).broadcast_to([8, 4, T // 4])
            )
        two_l = load_list("two_l", two)
        d_wd = load_words("d_wd", d_words, G)
        offs_l = load_list("offs_l", offs)
        k1_l = load_list("k1_l", k1)
        x_wd = load_words("x_wd", x_words, T)
        tau_t = load_rows(sb.tile([P, PACK], F32, name="tau_t")[:], tau)
        n1_l = load_list("n1_l", n1)
        n2_l = load_list("n2_l", n2)
        n3_l = load_list("n3_l", n3)

        row_win = [sb.tile([P, 2 * S], F32, name="row_win%d" % t) for t in range(PACK)]
        for t in range(PACK):
            nc.vector.memset(row_win[t][:, S:], 0.0)
        a_win = sb.tile([P, (PACK + 1) * S], F32, name="a_win")
        nc.vector.memset(a_win[:, PACK * S :], 0.0)

        def deal_scales(name, d_list, tag, plane):
            got = sb.tile([P, H], U8, name=name, tag=tag, align_bytes=64)
            nc.vector.tensor_copy(got[:], d_sc[:].indirect(d_list[:]))
            nc.vector.tensor_copy(
                plane[:, :H].rearrange("p (t c i) -> p c t i", t=PACK, i=16),
                got[:].rearrange("p (c i t) -> p c t i", t=PACK, i=16),
            )

        def place_scale_rows(queue, plane):
            for c in range(1, 4):
                queue.dma_start(plane[c:P:32, :].bitcast(I32), plane[8 * c : P : 32, :].bitcast(I32))

        def deal_words(got, dealt):
            nc.vector.tensor_copy(
                dealt[:].rearrange("p (t c i) -> p c t i", t=PACK, i=4),
                got.rearrange("p (c i t) -> p c t i", t=PACK, i=4),
            )

        def product(name, dealt, d_plane, x_got, x_plane):
            sums = [ps.tile([P, S], F32, name="%s_bank%d" % (name, t), tag="%s%d" % (name, t))[:] for t in range(PACK)]
            for t in range(PACK):
                cols = slice(t * P, (t + 1) * P)
                nc.tensor.matmul_mx(
                    out=sums[t], lhsT=dealt[:, cols].bitcast(FP8X4), lhsT_scale=d_plane[:, cols],
                    rhs=x_got.bitcast(FP8X4), rhs_scale=x_plane, start=True, stop=True,
                )
            return sums

        b_plane = sb.tile([P, H], U8, name="b_plane", align_bytes=64)
        deal_scales("b_dbytes", k2_l, "first", b_plane)
        place_scale_rows(nc.scalar, b_plane)
        x_bytes = sb.tile([P, 2 * S], U8, name="x_bytes", align_bytes=64)
        nc.vector.tensor_copy(x_bytes[:, :S], x_sc[:].indirect(two_l[:]))
        nc.vector.tensor_copy(x_bytes[:, S:], x_sc[:].indirect(offs_l[:]))

        rows = sb.tile([P, 4, 8], F32, name="rows", tag="first", align_bytes=64)
        gn_t, sl_t, lo_t, hi_t = [
            load_rows(rows[:, u, :PACK], src) for u, src in enumerate((gn, sl, lo, hi))
        ]

        b_dwords = sb.tile([P, H], U32, name="b_dwords", tag="third", align_bytes=64)
        b_xwords = sb.tile([P, S], U32, name="b_xwords", tag="second", align_bytes=64)
        b_dealt = sb.tile([P, H], U32, name="b_dealt", tag="fourth", align_bytes=64)
        nc.vector.tensor_copy(b_dwords[:], d_wd[:].indirect(k2_l[:]))
        nc.vector.tensor_copy(b_xwords[:], x_wd[:].indirect(two_l[:]))
        deal_words(b_dwords[:], b_dealt)
        w_raw = sb.tile([P, PACK, N], F32, name="w_raw", tag="third", align_bytes=64)
        nc.sync.dma_start(w_raw[:], w1.rearrange("(p j) m -> p j m", j=PACK))
        b_sums = product("b", b_dealt, b_plane, b_xwords[:], x_bytes[:, :S])

        top = sb.tile([P, PACK], F32, name="top")
        exp_bias = sb.tile([P, PACK], F32, name="exp_bias")
        ea = sb.tile([P, PACK, S], F32, name="ea")

        def empty_b(t):
            nc.vector.tensor_scalar(
                row_win[t][:, :S], b_sums[t], 0.0625, None, ALU.mult, ALU.max, accum_out=top[:, t : t + 1]
            )

        def fetch_exp(t):
            nc.vector.tensor_scalar(
                exp_bias[:, t : t + 1], top[:, t : t + 1], tau_t[:, t : t + 1], -1.0, ALU.mult, ALU.mult
            )
            nc.scalar.activation(
                ea[:, t, :], row_win[t][:].indirect(n1_l[:]), ACT.Exp,
                bias=exp_bias[:, t : t + 1], scale=tau_t[:, t : t + 1],
            )

        empty_b(0)
        for t in range(1, PACK):
            empty_b(t)
            fetch_exp(t - 1)
        fetch_exp(PACK - 1)

        a_plane = sb.tile([P, H], U8, name="a_plane", align_bytes=64)
        deal_scales("a_dbytes", k1_l, "second", a_plane)
        place_scale_rows(nc.sync, a_plane)
        a_dwords = sb.tile([P, H], U32, name="a_dwords", tag="second", align_bytes=64)
        a_xwords = sb.tile([P, S], U32, name="a_xwords", tag="fourth", align_bytes=64)
        a_dealt = sb.tile([P, H], U32, name="a_dealt", tag="a_dealt", align_bytes=64)
        nc.vector.tensor_copy(a_dwords[:], d_wd[:].indirect(k1_l[:]))
        nc.vector.tensor_copy(a_xwords[:], x_wd[:].indirect(offs_l[:]))
        deal_words(a_dwords[:], a_dealt)
        a_sums = product("a", a_dealt, a_plane, a_xwords[:], x_bytes[:, S:])

        gain = sb.tile([P, PACK], F32, name="gain")
        nc.gpsimd.tensor_scalar(gain[:], gn_t, 8.0 * 0.5 * 0.0625, 0.0, ALU.mult, ALU.add)
        neg_sl = sb.tile([P, PACK], F32, name="neg_sl")
        nc.gpsimd.tensor_scalar(neg_sl[:], sl_t, -1.0, 0.0, ALU.mult, ALU.add)
        lo_bias = sb.tile([P, PACK], F32, name="lo_bias")
        hi_bias = sb.tile([P, PACK], F32, name="hi_bias")
        nc.gpsimd.tensor_tensor(lo_bias[:], neg_sl[:], lo_t, ALU.mult)
        nc.gpsimd.tensor_tensor(hi_bias[:], neg_sl[:], hi_t, ALU.mult)

        w_bf = {}

        def round_weights(u, tag, copy):
            w_bf[u] = sb.tile([P, 2 * N], BF16, name="w_bf%d" % u, tag=tag, align_bytes=64)
            copy(
                w_bf[u][:].rearrange("p (t m j) -> p m j t", t=2, j=PACK),
                w_raw[:].rearrange("p j (m t) -> p m j t", t=PACK)[:, :, :, 2 * u : 2 * u + 2],
            )

        w_codes = sb.tile([P, N], U32, name="w_codes", align_bytes=64)
        w_plane = sb.tile([P, N], U8, name="w_plane", align_bytes=64)

        def quantize_weights(u):
            cols = slice(2 * u * P, 2 * (u + 1) * P)
            nc.vector.quantize_mx(out=w_codes[:, cols].bitcast(FP8X4), scales=w_plane[:, cols], in_=w_bf[u][:])

        def a_at(t):
            return (PACK - 1 - t) * S

        root = sb.tile([P, PACK, S], F32, name="root", tag="root", align_bytes=64)
        recip = sb.tile([P, PACK, S], F32, name="recip", tag="a_dealt", align_bytes=64)
        nc.scalar.activation(root[:], ea[:], ACT.Ln, scale=8.0, bias=1.0)
        round_weights(0, "second", nc.vector.tensor_copy)
        quantize_weights(0)
        for t in range(PACK):
            nc.scalar.activation(a_win[:, a_at(t) : a_at(t) + S], a_sums[t], ACT.Copy, scale=gain[:, t : t + 1])
        halves = [slice(u * S // 2, (u + 1) * S // 2) for u in range(2)]
        for cols in halves:
            nc.scalar.activation(recip[:, :, cols], root[:, :, cols], ACT.Sigmoid, scale=-1.0)

        round_weights(1, "root", nc.scalar.copy)

        a_got = sb.tile([P, PACK, S], F32, name="a_got")
        diff = sb.tile([P, PACK, S], F32, name="diff")
        for t in range(PACK):
            nc.vector.tensor_copy(a_got[:, t, :], a_win[:, a_at(t) : a_at(t) + 2 * S].indirect(n2_l[:]))
        for t in range(PACK):
            nc.vector.scalar_tensor_tensor(
                diff[:, t, :], a_sums[t], gain[:, t : t + 1], a_got[:, t, :], ALU.mult, ALU.subtract
            )

        z_bf = sb.tile([P, S, PACK], BF16, name="z_bf", align_bytes=64)
        z_codes = sb.tile([P, S], U32, name="z_codes", align_bytes=64)
        z_plane = sb.tile([P, S], U8, name="z_plane", align_bytes=64)
        for cols in halves:
            nc.vector.tensor_tensor(
                z_bf[:, cols, :].rearrange("p (c i) t -> p c t i", i=4),
                diff[:, :, cols].rearrange("p t (c i) -> p c t i", i=4),
                recip[:, :, cols].rearrange("p t (c i) -> p c t i", i=4),
                ALU.mult,
            )
        for cols in halves:
            nc.vector.quantize_mx(
                out=z_codes[:, cols].bitcast(FP8X4), scales=z_plane[:, cols],
                in_=z_bf[:, cols, :].rearrange("p j t -> p (j t)"),
            )
        quantize_weights(1)

        out_rows = out.rearrange("(p t) j -> p t j", t=PACK)
        h_sums = [ps.tile([P, S], F32, name="h_bank%d" % t, tag="b%d" % t) for t in range(PACK)]
        for t in range(PACK):
            cols = slice(t * P, (t + 1) * P)
            nc.tensor.matmul_mx(
                out=h_sums[t][:], lhsT=w_codes[:, cols].bitcast(FP8X4), lhsT_scale=w_plane[:, cols],
                rhs=z_codes[:].bitcast(FP8X4), rhs_scale=z_plane[:], start=True, stop=True,
            )
        for t in range(PACK):
            nc.vector.tensor_copy(row_win[t][:, :S], h_sums[t][:])
        for t in range(PACK):
            sg = sb.tile([P, S], F32, name="sg%d" % t)
            sg2 = sb.tile([P, S], F32, name="sg2%d" % t)
            band = sb.tile([P, S], F32, name="band%d" % t)
            result = sb.tile([P, S], F32, name="result%d" % t)
            slope = sl_t[:, t : t + 1]
            nc.scalar.activation(
                sg[:], row_win[t][:].indirect(n3_l[:]), ACT.Sigmoid, bias=lo_bias[:, t : t + 1], scale=slope
            )
            for cols in halves if t == PACK - 1 else [slice(0, S)]:
                places = n3_l[:, cols.start // 16 : cols.stop // 16]
                nc.scalar.activation(
                    sg2[:, cols], row_win[t][:].indirect(places), ACT.Sigmoid, bias=hi_bias[:, t : t + 1], scale=slope
                )
                nc.vector.tensor_tensor(band[:, cols], sg[:, cols], sg2[:, cols], ALU.subtract)
                nc.vector.tensor_tensor(result[:, cols], band[:, cols], h_sums[t][:, cols], ALU.mult)
                nc.sync.dma_start(out_rows[:, t, cols], result[:, cols])
